import numpy as np
import ml_dtypes


def mxq(x, axis, fmt="e4m3"):
    dtype, down = {"e4m3": (ml_dtypes.float8_e4m3fn, 7), "e5m2": (ml_dtypes.float8_e5m2, 14)}[fmt]
    v = np.moveaxis(np.asarray(x, np.float32).astype(ml_dtypes.bfloat16).astype(np.float64), axis, -1)
    blocks = v.reshape(v.shape[:-1] + (-1, 32))
    amax = np.abs(blocks).max(-1, keepdims=True)
    byte = np.maximum(np.where(amax > 0, np.frexp(amax)[1] - 1 + 127, 0) - down, 1)
    scale = np.exp2(byte - 127.0)
    codes = (blocks / scale).astype(np.float32).astype(dtype).astype(np.float64)
    return np.moveaxis((codes * scale).reshape(v.shape), -1, axis)


WIDE = False


def mx_kscale(k):
    if not WIDE:
        return np.ones(k)
    levels = np.array([10, -10, 5, -5, 0])
    if k % 512:
        return np.exp2(np.random.permutation(np.resize(levels, k // 32))).repeat(32)
    a = np.empty((k // 512, 16))
    for p in range(k // 512):
        a[p, :8] = np.random.permutation(np.resize(levels, 8))
        for g in range(8):
            far = levels[np.abs(levels - a[p, g]) >= 10]
            a[p, g + 8] = far[np.random.randint(len(far))]
    return np.exp2(a.ravel()).repeat(32)


def f64(x):
    return np.asarray(x).astype(np.float64)


def striped(idx):
    return np.tile(idx.reshape(-1, 16).T, (8, 1)).astype(np.uint16)


def unstriped(offs):
    return offs[:16].T.reshape(-1).astype(np.int64)


E2M1 = np.array([0.0, 0.5, 1.0, 1.5, 2.0, 3.0, 4.0, 6.0, -0.0, -0.5, -1.0, -1.5, -2.0, -3.0, -4.0, -6.0])


def pack_weight(w, fmt):
    k, n = w.shape
    w = f64(np.asarray(w, np.float32).astype(ml_dtypes.bfloat16)).reshape(k // 32, 32, n)
    amax = np.abs(w).max(1)
    if fmt == "e4m3":
        byte = np.frexp(amax)[1] - 1 + 127 - 7
    else:
        mant, ex = np.frexp(amax / 6.0)
        byte = np.where(mant > 0.5, ex, ex - 1) + 127
    byte = np.clip(np.where(amax > 0, byte, 1), 1, 254)
    scaled = (w * np.exp2(127.0 - byte)[:, None, :]).reshape(k, n).astype(np.float32)
    by_word = np.ascontiguousarray(scaled.reshape(k // 512, 128, 4, n).transpose(0, 1, 3, 2))
    if fmt == "e4m3":
        words = by_word.astype(ml_dtypes.float8_e4m3fn).view(np.uint8)
    else:
        c = by_word.astype(ml_dtypes.float4_e2m1fn).view(np.uint8) & 0xF
        words = (c[..., 0::2] | (c[..., 1::2] << 4)).reshape(k // 512, 128, 2 * n)
    return np.ascontiguousarray(words), np.ascontiguousarray(byte.astype(np.uint8).reshape(k // 512, 16, n))


def unpack_weight(words, scales, fmt):
    g, _, n = scales.shape
    words = np.ascontiguousarray(words).reshape(g, 128, n, -1)
    if fmt == "e4m3":
        vals = words.view(ml_dtypes.float8_e4m3fn).astype(np.float64)
    else:
        nib = np.empty((g, 128, n, 4), np.uint8)
        nib[..., 0::2] = words & 0xF
        nib[..., 1::2] = words >> 4
        vals = E2M1[nib]
    vals = vals * np.repeat(np.exp2(scales.astype(np.float64) - 127.0), 8, axis=1)[..., None]
    return vals.transpose(0, 1, 3, 2).reshape(g * 512, n)


def d_relu2(v):
    return 2.0 * np.maximum(v, 0.0)


K, T, E, C, H, N = 384, 768, 6, 256, 1024, 512


def by_expert(wq, xq):
    return np.concatenate([wq[e].T @ xq[:, e * C:(e + 1) * C] for e in range(E)], axis=1)


def setup_inputs():
    n = np.random.standard_normal
    s = mx_kscale(N)[:, None]
    u = mx_kscale(H)
    first = np.random.permutation(np.repeat(np.arange(E), T // E))
    second = (first + 1 + np.random.permutation(np.repeat(np.arange(E - 1), -(-T // (E - 1)))[:T])) % E
    while np.bincount(second, minlength=E).max() != T // E:
        load = np.bincount(second, minlength=E); hi, lo = int(load.argmax()), int(load.argmin())
        t = np.flatnonzero((second == hi) & (first != lo))[0]; second[t] = lo
    slot_token = np.empty(E * C, np.int64); pos = np.empty((2, T), np.int64); fill = np.zeros(E, np.int64)
    place = np.stack([np.random.permutation(C) for _ in range(E)])
    for r, deal in enumerate((first, second)):
        for t in np.random.permutation(T):
            e = deal[t]; j = e * C + place[e, fill[e]]; fill[e] += 1; slot_token[j] = t; pos[r, t] = j
    g = np.random.uniform(0.2, 0.8, T)
    w_slot = np.empty(E * C); w_slot[pos[0]] = g; w_slot[pos[1]] = 1.0 - g
    w2 = [pack_weight(m, "e2m1") for m in n((E, N, H)) / np.sqrt(N) / s[None] * u[None, None, :]]
    w1 = [pack_weight(m, "e2m1") for m in n((E, H, K)) / np.sqrt(H) / u[None, :, None]]
    return {
        "dyT": (n((N, T)) * s).astype(np.float32),
        "a": n((H, E * C)).astype(np.float32),
        "w2_words": np.stack([m[0] for m in w2]),
        "w2_scales": np.stack([m[1] for m in w2]),
        "w1_words": np.stack([m[0] for m in w1]),
        "w1_scales": np.stack([m[1] for m in w1]),
        "gate": np.tile(w_slot, (N, 1)).astype(np.float32),
        "offs": striped(slot_token),
        "pos1": striped(pos[0]),
        "pos2": striped(pos[1]),
    }


def reference(dyT, a, w2_words, w2_scales, w1_words, w1_scales, gate, offs, pos1, pos2):
    idx = unstriped(offs)
    w2 = np.stack([unpack_weight(w2_words[e], w2_scales[e], "e2m1") for e in range(E)])
    w1 = np.stack([unpack_weight(w1_words[e], w1_scales[e], "e2m1") for e in range(E)])
    gq = mxq(f64(gate) * f64(dyT)[:, idx], 0, "e4m3")
    dh = by_expert(w2, gq)
    da = dh * d_relu2(f64(a))
    dx = by_expert(w1, mxq(da, 0, "e4m3"))
    return dx[:, unstriped(pos1)] + dx[:, unstriped(pos2)]

@@ -1,0 +1,306 @@
+from contextlib import ExitStack
+
+import concourse.mybir as mybir
+
+K, T, E, C, H, N = 384, 768, 6, 256, 1024, 512
+S = E * C
+P = 128
+PACK = 4
+PASSES = H // (P * PACK)
+KT = K // P
+PAIR = 2 * C
+HALF = 128
+
+F32 = mybir.dt.float32
+BF16 = mybir.dt.bfloat16
+I32 = mybir.dt.int32
+U32 = mybir.dt.uint32
+U16 = mybir.dt.uint16
+U8 = mybir.dt.uint8
+FP8X4 = mybir.dt.float8_e4m3fn_x4
+FP4X4 = mybir.dt.float4_e2m1fn_x4
+MULT = mybir.AluOpType.mult
+ADD = mybir.AluOpType.add
+RELU = mybir.ActivationFunctionType.Relu
+
+FLOPS = 2 * S * (N * H + H * K)
+BYTES = 4 * (N * T + H * S + S + K * T) + E * (N * H + H * K) // 2 + E * (N * H + H * K) // 32 + 2 * P * (S + 2 * T) // 16
+
+
+def tile_moe_bdx_mlp_relu2_kernel(
+    tc, dyT, a, w2_words, w2_scales, w1_words, w1_scales, gate, offs, pos1, pos2, out
+):
+    nc = tc.nc
+    with ExitStack() as ctx:
+        keep = ctx.enter_context(tc.tile_pool(name="keep", bufs=1))
+        ring = ctx.enter_context(tc.tile_pool(name="ring", bufs=3))
+        relu_ring = ctx.enter_context(tc.tile_pool(name="relu_ring", bufs=4))
+        dh_banks = ctx.enter_context(tc.psum_pool(name="dh_banks", bufs=5))
+        dx_banks = ctx.enter_context(tc.psum_pool(name="dx_banks", bufs=3))
+
+        offs_sb = keep.tile([P, S // 16], U16, name="offs_sb")
+        pos_sb = [keep.tile([P, T // 16], U16, name=f"pos_sb{r}") for r in range(2)]
+        dy_sb = [keep.tile([P, T], F32, name=f"dy_sb{t}") for t in range(PACK)]
+        gate_sb = [keep.tile([P, PAIR], F32, name=f"gate_sb{c}") for c in range(E // 2)]
+        a_sb = [[keep.tile([P, PACK, PAIR], F32, name=f"a_sb{c}_{s}") for s in range(PASSES)] for c in range(E // 2)]
+        w2_raw = [keep.tile([P, 2, 2 * H], U8, name=f"w2_raw{c}") for c in range(E // 2)]
+        w2_sb = [keep.tile([P, 2, 2 * H], U8, name=f"w2_sb{c}", align_bytes=64) for c in range(E // 2)]
+        w1_sb = [keep.tile([P, 2 * PASSES, 2 * K], U8, name=f"w1_sb{c}", align_bytes=64) for c in range(E // 2)]
+        w2s_raw = keep.tile([P, H], U8, name="w2s_raw")
+        w2s_turned = keep.tile([P, H], U8, name="w2s_turned")
+        w2s_sb = keep.tile([P, E * H], U8, name="w2s_sb", align_bytes=64)
+        w1s_sb = keep.tile([P, E * PASSES * K], U8, name="w1s_sb", align_bytes=64)
+        dx_sb = [keep.tile([P, S], F32, name=f"dx_sb{kt}") for kt in range(KT)]
+        warm = keep.tile([P, 2], F32, name="warm")
+
+        dy_rows = dyT.rearrange("(p t) j -> p t j", t=PACK)
+        a_rows = a.rearrange("(s p t) j -> s p t j", s=PASSES, t=PACK)
+
+        def load_gate(c):
+            nc.sync.dma_start(gate_sb[c][:], gate[0:P, c * PAIR : (c + 1) * PAIR])
+
+        def load_w2(c):
+            nc.sync.dma_start(
+                w2_raw[c][:].bitcast(I32),
+                w2_words[2 * c : 2 * c + 2].rearrange("e o p b -> p (e o) b").bitcast(I32),
+            )
+
+        def load_w1(c):
+            nc.sync.dma_start(
+                w1_sb[c][:].bitcast(I32),
+                w1_words[2 * c : 2 * c + 2].rearrange("e s p b -> p (e s) b").bitcast(I32),
+            )
+
+        def load_a(c):
+            for s in range(PASSES):
+                nc.sync.dma_start(a_sb[c][s][:], a_rows[s][:, :, c * PAIR : (c + 1) * PAIR])
+
+        scale_groups = ((0, 4, 0), (4, 2, 64))
+
+        nc.vector.memset(w2s_raw[64:P, :].bitcast(I32), 0)
+        nc.vector.memset(w2s_sb[:].bitcast(I32), 0)
+        nc.vector.memset(w1s_sb[:].bitcast(I32), 0)
+        nc.vector.memset(warm[:], 0.0)
+        nc.scalar.activation(warm[:, 1:2], warm[:, 0:1], RELU)
+
+        nc.sync.dma_start(offs_sb[:], offs)
+        nc.sync.dma_start(dy_sb[0][:], dy_rows[:, 0, :])
+        load_gate(0)
+        for e0, ne, p0 in scale_groups:
+            nc.sync.dma_start(
+                w2s_raw[p0 : p0 + 16 * ne, :].bitcast(I32),
+                w2_scales[e0 : e0 + ne].rearrange("e o f i -> f (e o) i").bitcast(I32),
+            )
+        for t in range(1, PACK):
+            nc.sync.dma_start(dy_sb[t][:], dy_rows[:, t, :])
+        load_gate(1)
+        load_w2(0)
+        load_a(0)
+        load_gate(2)
+        load_w1(0)
+        for q in range(4):
+            nc.sync.dma_start(
+                w1s_sb[32 * q : 32 * q + 4, :].rearrange("f (g k) -> f g k", k=K).bitcast(I32),
+                w1_scales[:, :, 4 * q : 4 * q + 4, :].rearrange("e s f k -> f (e s) k").bitcast(I32),
+            )
+        load_w2(1)
+        load_a(1)
+        load_w1(1)
+        load_w2(2)
+        load_a(2)
+        load_w1(2)
+        nc.sync.dma_start(pos_sb[0][:], pos1)
+        nc.sync.dma_start(pos_sb[1][:], pos2)
+
+        g_rows, g_bf, g_codes, g_scales = {}, {}, {}, {}
+        relu_sb, da_bf, da_codes, da_scales = {}, {}, {}, {}
+
+        def gather_g(c, t):
+            if t == 0:
+                g_rows[c] = ring.tile([P, PACK, PAIR], F32, name="g_rows")
+            cols = PAIR // 16
+            nc.vector.tensor_tensor(
+                g_rows[c][:, t, :], dy_sb[t][:].indirect(offs_sb[:, c * cols : (c + 1) * cols]), gate_sb[c][:], MULT
+            )
+
+        def round_g(e):
+            g_bf[e] = ring.tile([P, C, PACK], BF16, name="g_bf", align_bytes=64)
+            src = g_rows[e // 2][:, :, (e % 2) * C : (e % 2 + 1) * C]
+            nc.scalar.copy(
+                g_bf[e][:].rearrange("p (c i) t -> p c t i", i=2), src.rearrange("p t (c i) -> p c t i", i=2)
+            )
+
+        def quantize_g(e):
+            g_codes[e] = ring.tile([P, C], U32, name="g_codes", align_bytes=64)
+            g_scales[e] = ring.tile([P, C], U8, name="g_scales", align_bytes=64)
+            nc.vector.quantize_mx(
+                out=g_codes[e][:].bitcast(FP8X4), scales=g_scales[e][:], in_=g_bf[e][:].rearrange("p c t -> p (c t)")
+            )
+
+        def turn_w2(c):
+            nc.vector.tensor_copy(
+                w2_sb[c][:].bitcast(U16).rearrange("p e (s t m) -> p (e s) t m", s=PASSES, t=PACK),
+                w2_raw[c][:].bitcast(U16).rearrange("p e (s m t) -> p (e s) t m", s=PASSES, t=PACK),
+            )
+
+        def turn_w2_scales():
+            nc.vector.tensor_copy(
+                w2s_turned[:].rearrange("p (s t m) -> p s t m", s=PASSES, t=PACK),
+                w2s_raw[:].rearrange("p (s m t) -> p s t m", s=PASSES, t=PACK),
+            )
+            for e0, ne, p0 in scale_groups:
+                for q in range(4):
+                    nc.scalar.dma_start(
+                        w2s_sb[32 * q : 32 * q + 4, e0 * H : (e0 + ne) * H].bitcast(I32),
+                        w2s_turned[p0 + 4 * ne * q : p0 + 4 * ne * (q + 1), :].bitcast(I32),
+                    )
+
+        def relu_a(e, s):
+            relu_sb[e, s] = relu_ring.tile([P, C, PACK], F32, name="relu_sb")
+            src = a_sb[e // 2][s][:, :, (e % 2) * C : (e % 2 + 1) * C]
+            nc.scalar.activation(
+                relu_sb[e, s][:].rearrange("p (c i) t -> p c t i", i=2),
+                src.rearrange("p t (c i) -> p c t i", i=2),
+                RELU,
+                scale=2.0,
+            )
+
+        def make_da(e, h, s):
+            if h == 0 and s == 0:
+                da_bf[e] = ring.tile([P, 2, PASSES, HALF, PACK], BF16, name="da_bf", align_bytes=64)
+                da_codes[e] = ring.tile([P, 2, PASSES, HALF], U32, name="da_codes", align_bytes=64)
+                da_scales[e] = ring.tile([P, 2, PASSES, HALF], U8, name="da_scales", align_bytes=64)
+            dh = dh_banks.tile([P, PACK, HALF], F32, name="dh")
+            slots = slice(h * HALF, (h + 1) * HALF)
+            for t in range(PACK):
+                col = (s * PACK + t) * P
+                nc.tensor.matmul_mx(
+                    out=dh[:, t, :],
+                    lhsT=w2_sb[e // 2][:, e % 2, 2 * col : 2 * (col + P)].bitcast(FP4X4),
+                    lhsT_scale=w2s_sb[:, e * H + col : e * H + col + P],
+                    rhs=g_codes[e][:, slots].bitcast(FP8X4),
+                    rhs_scale=g_scales[e][:, slots],
+                    start=True,
+                    stop=True,
+                )
+            nc.vector.tensor_tensor(
+                da_bf[e][:, h, s, :, :], dh[:].rearrange("p t n -> p n t"), relu_sb[e, s][:, slots, :], MULT
+            )
+
+        def quantize_da(e, first, count):
+            words = slice(first * HALF, (first + count) * HALF)
+            values = slice(first * HALF * PACK, (first + count) * HALF * PACK)
+            nc.vector.quantize_mx(
+                out=da_codes[e][:].rearrange("p h s n -> p (h s n)")[:, words].bitcast(FP8X4),
+                scales=da_scales[e][:].rearrange("p h s n -> p (h s n)")[:, words],
+                in_=da_bf[e][:].rearrange("p h s n t -> p (h s n t)")[:, values],
+            )
+
+        def make_dx(e, halves):
+            for kt in range(KT):
+                dx = dx_banks.tile([P, C], F32, name="dx")
+                for h in halves:
+                    for s in range(PASSES):
+                        group = (e % 2) * PASSES + s
+                        col = (e * PASSES + s) * K + kt * P
+                        nc.tensor.matmul_mx(
+                            out=dx[:, h * HALF : (h + 1) * HALF],
+                            lhsT=w1_sb[e // 2][:, group, 2 * kt * P : 2 * (kt + 1) * P].bitcast(FP4X4),
+                            lhsT_scale=w1s_sb[:, col : col + P],
+                            rhs=da_codes[e][:, h, s, :].bitcast(FP8X4),
+                            rhs_scale=da_scales[e][:, h, s, :],
+                            start=(s == 0),
+                            stop=(s == PASSES - 1),
+                        )
+                lo, hi = halves[0] * HALF, (halves[-1] + 1) * HALF
+                nc.scalar.copy(dx_sb[kt][:, e * C + lo : e * C + hi], dx[:, lo:hi])
+
+        def expert(e):
+            for h in range(2):
+                for s in range(PASSES):
+                    make_da(e, h, s)
+
+        gather_g(0, 0)
+        turn_w2_scales()
+        for t in range(1, PACK):
+            gather_g(0, t)
+        round_g(0)
+        round_g(1)
+        gather_g(1, 0)
+        turn_w2(0)
+        quantize_g(0)
+        gather_g(1, 1)
+        gather_g(1, 2)
+        quantize_g(1)
+        gather_g(1, 3)
+        for s in range(PASSES):
+            relu_a(0, s)
+        for s in range(PASSES):
+            relu_a(1, s)
+        round_g(2)
+        round_g(3)
+        expert(0)
+        turn_w2(1)
+        quantize_da(0, 0, 4)
+        make_dx(0, (0, 1))
+        expert(1)
+        quantize_g(2)
+        quantize_da(1, 0, 4)
+        make_dx(1, (0, 1))
+        quantize_g(3)
+        for s in range(PASSES):
+            relu_a(2, s)
+        for t in range(PACK):
+            gather_g(2, t)
+        for s in range(PASSES):
+            relu_a(3, s)
+        round_g(4)
+        round_g(5)
+        expert(2)
+        turn_w2(2)
+        quantize_da(2, 0, 4)
+        make_dx(2, (0, 1))
+        for s in range(PASSES):
+            relu_a(4, s)
+        expert(3)
+        quantize_g(4)
+        quantize_da(3, 0, 4)
+        make_dx(3, (0, 1))
+        quantize_g(5)
+        for s in range(PASSES):
+            relu_a(5, s)
+        expert(4)
+        last = E - 1
+        make_da(last, 0, 0)
+        quantize_da(4, 0, 4)
+        make_dx(4, (0, 1))
+        make_da(last, 0, 1)
+        make_da(last, 1, 0)
+        quantize_da(last, 0, 2)
+        make_dx(last, (0,))
+        make_da(last, 1, 1)
+        quantize_da(last, 2, 1)
+        quantize_da(last, 3, 1)
+        make_dx(last, (1,))
+
+        pieces = [(0, 0, T), (1, 0, T), (2, 0, T // 2), (2, T // 2, T)]
+        picked = {}
+
+        def pick(n, r):
+            kt, lo, hi = pieces[n]
+            picked[n, r] = keep.tile([P, hi - lo], F32, name=f"picked{n}_{r}")
+            nc.vector.tensor_copy(picked[n, r][:], dx_sb[kt][:].indirect(pos_sb[r][:, lo // 16 : hi // 16]))
+
+        def combine(n):
+            kt, lo, hi = pieces[n]
+            total = keep.tile([P, hi - lo], F32, name=f"total{n}")
+            nc.vector.tensor_tensor(total[:], picked[n, 0][:], picked[n, 1][:], ADD)
+            nc.sync.dma_start(out[kt * P : (kt + 1) * P, lo:hi], total[:])
+
+        pick(0, 0)
+        pick(0, 1)
+        for n in range(1, len(pieces)):
+            pick(n, 0)
+            combine(n - 1)
+            pick(n, 1)
+        combine(len(pieces) - 1)

@@ -1,6 +1,7 @@
 from contextlib import ExitStack
 
 import concourse.mybir as mybir
+from concourse.masks import make_identity
 
 K, T, E, C, H, N = 384, 768, 6, 256, 1024, 512
 S = E * C
@@ -34,9 +35,10 @@ def tile_moe_bdx_mlp_relu2_kernel(
     with ExitStack() as ctx:
         keep = ctx.enter_context(tc.tile_pool(name="keep", bufs=1))
         ring = ctx.enter_context(tc.tile_pool(name="ring", bufs=3))
-        relu_ring = ctx.enter_context(tc.tile_pool(name="relu_ring", bufs=4))
-        dh_banks = ctx.enter_context(tc.psum_pool(name="dh_banks", bufs=5))
-        dx_banks = ctx.enter_context(tc.psum_pool(name="dx_banks", bufs=3))
+        single = ctx.enter_context(tc.tile_pool(name="single", bufs=1))
+        relu_ring = ctx.enter_context(tc.tile_pool(name="relu_ring", bufs=6))
+        dh_banks = ctx.enter_context(tc.psum_pool(name="dh_banks", bufs=6))
+        dx_banks = ctx.enter_context(tc.psum_pool(name="dx_banks", bufs=2))
 
         offs_sb = keep.tile([P, S // 16], U16, name="offs_sb")
         pos_sb = [keep.tile([P, T // 16], U16, name=f"pos_sb{r}") for r in range(2)]
@@ -50,8 +52,11 @@ def tile_moe_bdx_mlp_relu2_kernel(
         w2s_turned = keep.tile([P, H], U8, name="w2s_turned")
         w2s_sb = keep.tile([P, E * H], U8, name="w2s_sb", align_bytes=64)
         w1s_sb = keep.tile([P, E * PASSES * K], U8, name="w1s_sb", align_bytes=64)
-        dx_sb = [keep.tile([P, S], F32, name=f"dx_sb{kt}") for kt in range(KT)]
+        dx_sb = keep.tile([P, KT, S], F32, name="dx_sb")
         warm = keep.tile([P, 2], F32, name="warm")
+
+        ident = keep.tile([P, P], F32, name="ident")
+        make_identity(nc, ident[:])
 
         dy_rows = dyT.rearrange("(p t) j -> p t j", t=PACK)
         a_rows = a.rearrange("(s p t) j -> s p t j", s=PASSES, t=PACK)
@@ -71,68 +76,66 @@ def tile_moe_bdx_mlp_relu2_kernel(
                 w1_words[2 * c : 2 * c + 2].rearrange("e s p b -> p (e s) b").bitcast(I32),
             )
 
-        def load_a(c):
-            for s in range(PASSES):
-                nc.sync.dma_start(a_sb[c][s][:], a_rows[s][:, :, c * PAIR : (c + 1) * PAIR])
+        def load_a(c, s, lo=0, hi=PAIR):
+            nc.sync.dma_start(a_sb[c][s][:, :, lo:hi], a_rows[s][:, :, c * PAIR + lo : c * PAIR + hi])
 
-        scale_groups = ((0, 4, 0), (4, 2, 64))
-
-        nc.vector.memset(w2s_raw[64:P, :].bitcast(I32), 0)
+        nc.vector.memset(w2s_raw[96:P, :].bitcast(I32), 0)
         nc.vector.memset(w2s_sb[:].bitcast(I32), 0)
         nc.vector.memset(w1s_sb[:].bitcast(I32), 0)
+        nc.scalar.dma_start(
+            w2s_raw[0 : 16 * E, :].bitcast(I32), w2_scales.rearrange("e o f i -> f (e o) i").bitcast(I32)
+        )
         nc.vector.memset(warm[:], 0.0)
         nc.scalar.activation(warm[:, 1:2], warm[:, 0:1], RELU)
-
         nc.sync.dma_start(offs_sb[:], offs)
         nc.sync.dma_start(dy_sb[0][:], dy_rows[:, 0, :])
         load_gate(0)
-        for e0, ne, p0 in scale_groups:
-            nc.sync.dma_start(
-                w2s_raw[p0 : p0 + 16 * ne, :].bitcast(I32),
-                w2_scales[e0 : e0 + ne].rearrange("e o f i -> f (e o) i").bitcast(I32),
-            )
         for t in range(1, PACK):
             nc.sync.dma_start(dy_sb[t][:], dy_rows[:, t, :])
         load_gate(1)
         load_w2(0)
-        load_a(0)
         load_gate(2)
-        load_w1(0)
+        load_a(0, 0)
+        load_a(0, 1)
         for q in range(4):
             nc.sync.dma_start(
                 w1s_sb[32 * q : 32 * q + 4, :].rearrange("f (g k) -> f g k", k=K).bitcast(I32),
                 w1_scales[:, :, 4 * q : 4 * q + 4, :].rearrange("e s f k -> f (e s) k").bitcast(I32),
             )
         load_w2(1)
-        load_a(1)
-        load_w1(1)
+        load_a(1, 0)
+        load_a(1, 1)
+        load_w1(0)
         load_w2(2)
-        load_a(2)
+        for half in range(2):
+            for s in range(PASSES):
+                load_a(2, s, half * C, (half + 1) * C)
+        load_w1(1)
         load_w1(2)
         nc.sync.dma_start(pos_sb[0][:], pos1)
         nc.sync.dma_start(pos_sb[1][:], pos2)
 
         g_rows, g_bf, g_codes, g_scales = {}, {}, {}, {}
-        relu_sb, da_bf, da_codes, da_scales = {}, {}, {}, {}
+        relu_sb, dh_sb, da_bf, da_codes, da_scales = {}, {}, {}, {}, {}
 
         def gather_g(c, t):
             if t == 0:
-                g_rows[c] = ring.tile([P, PACK, PAIR], F32, name="g_rows")
+                g_rows[c] = ring.tile([P, PACK, PAIR], F32, name="g_rows", tag="rows")
             cols = PAIR // 16
             nc.vector.tensor_tensor(
                 g_rows[c][:, t, :], dy_sb[t][:].indirect(offs_sb[:, c * cols : (c + 1) * cols]), gate_sb[c][:], MULT
             )
 
         def round_g(e):
-            g_bf[e] = ring.tile([P, C, PACK], BF16, name="g_bf", align_bytes=64)
+            g_bf[e] = keep.tile([P, C, PACK], BF16, name=f"g_bf{e}", align_bytes=64)
             src = g_rows[e // 2][:, :, (e % 2) * C : (e % 2 + 1) * C]
             nc.scalar.copy(
                 g_bf[e][:].rearrange("p (c i) t -> p c t i", i=2), src.rearrange("p t (c i) -> p c t i", i=2)
             )
 
         def quantize_g(e):
-            g_codes[e] = ring.tile([P, C], U32, name="g_codes", align_bytes=64)
-            g_scales[e] = ring.tile([P, C], U8, name="g_scales", align_bytes=64)
+            g_codes[e] = keep.tile([P, C], U32, name=f"g_codes{e}", align_bytes=64)
+            g_scales[e] = keep.tile([P, C], U8, name=f"g_scales{e}", align_bytes=64)
             nc.vector.quantize_mx(
                 out=g_codes[e][:].bitcast(FP8X4), scales=g_scales[e][:], in_=g_bf[e][:].rearrange("p c t -> p (c t)")
             )
@@ -148,12 +151,11 @@ def tile_moe_bdx_mlp_relu2_kernel(
                 w2s_turned[:].rearrange("p (s t m) -> p s t m", s=PASSES, t=PACK),
                 w2s_raw[:].rearrange("p (s m t) -> p s t m", s=PASSES, t=PACK),
             )
-            for e0, ne, p0 in scale_groups:
-                for q in range(4):
-                    nc.scalar.dma_start(
-                        w2s_sb[32 * q : 32 * q + 4, e0 * H : (e0 + ne) * H].bitcast(I32),
-                        w2s_turned[p0 + 4 * ne * q : p0 + 4 * ne * (q + 1), :].bitcast(I32),
-                    )
+            for q in range(4):
+                nc.gpsimd.dma_start(
+                    w2s_sb[32 * q : 32 * q + 4, :].bitcast(I32),
+                    w2s_turned[4 * E * q : 4 * E * (q + 1), :].bitcast(I32),
+                )
 
         def relu_a(e, s):
             relu_sb[e, s] = relu_ring.tile([P, C, PACK], F32, name="relu_sb")
@@ -165,12 +167,8 @@ def tile_moe_bdx_mlp_relu2_kernel(
                 scale=2.0,
             )
 
-        def make_da(e, h, s):
-            if h == 0 and s == 0:
-                da_bf[e] = ring.tile([P, 2, PASSES, HALF, PACK], BF16, name="da_bf", align_bytes=64)
-                da_codes[e] = ring.tile([P, 2, PASSES, HALF], U32, name="da_codes", align_bytes=64)
-                da_scales[e] = ring.tile([P, 2, PASSES, HALF], U8, name="da_scales", align_bytes=64)
-            dh = dh_banks.tile([P, PACK, HALF], F32, name="dh")
+        def make_dh(e, h, s):
+            dh = dh_banks.tile([P, PACK, HALF], F32, name="dh", tag="bank")
             slots = slice(h * HALF, (h + 1) * HALF)
             for t in range(PACK):
                 col = (s * PACK + t) * P
@@ -183,118 +181,139 @@ def tile_moe_bdx_mlp_relu2_kernel(
                     start=True,
                     stop=True,
                 )
-            nc.vector.tensor_tensor(
-                da_bf[e][:, h, s, :, :], dh[:].rearrange("p t n -> p n t"), relu_sb[e, s][:, slots, :], MULT
-            )
+            return dh[:].rearrange("p t n -> p n t")
 
-        def quantize_da(e, first, count):
-            words = slice(first * HALF, (first + count) * HALF)
-            values = slice(first * HALF * PACK, (first + count) * HALF * PACK)
+        def stage_dh(e):
+            dh_sb[e] = ring.tile([P, HALF, PACK], F32, name="dh_sb")
+            nc.scalar.copy(dh_sb[e][:], make_dh(e, 0, 0))
+
+        def make_da(e, h, s, engine):
+            if (e, h) not in da_bf:
+                pool = ring
+                da_bf[e, h] = pool.tile([P, PASSES, HALF, PACK], BF16, name=f"da_bf{h}", align_bytes=64)
+            dh = dh_sb[e][:] if engine is nc.gpsimd else make_dh(e, h, s)
+            engine.tensor_tensor(da_bf[e, h][:, s, :, :], dh, relu_sb[e, s][:, h * HALF : (h + 1) * HALF, :], MULT)
+
+        def quantize_da(e, h):
+            da_codes[e, h] = ring.tile([P, PASSES, HALF], U32, name=f"da_codes{h}", align_bytes=64)
+            da_scales[e, h] = ring.tile([P, PASSES, HALF], U8, name=f"da_scales{h}", align_bytes=64)
             nc.vector.quantize_mx(
-                out=da_codes[e][:].rearrange("p h s n -> p (h s n)")[:, words].bitcast(FP8X4),
-                scales=da_scales[e][:].rearrange("p h s n -> p (h s n)")[:, words],
-                in_=da_bf[e][:].rearrange("p h s n t -> p (h s n t)")[:, values],
+                out=da_codes[e, h][:].rearrange("p s n -> p (s n)").bitcast(FP8X4),
+                scales=da_scales[e, h][:].rearrange("p s n -> p (s n)"),
+                in_=da_bf[e, h][:].rearrange("p s n t -> p (s n t)"),
             )
 
-        def make_dx(e, halves):
+        def dx_passes(e, h, kt, dx):
+            for s in range(PASSES):
+                group = (e % 2) * PASSES + s
+                col = (e * PASSES + s) * K + kt * P
+                nc.tensor.matmul_mx(
+                    out=dx,
+                    lhsT=w1_sb[e // 2][:, group, 2 * kt * P : 2 * (kt + 1) * P].bitcast(FP4X4),
+                    lhsT_scale=w1s_sb[:, col : col + P],
+                    rhs=da_codes[e, h][:, s, :].bitcast(FP8X4),
+                    rhs_scale=da_scales[e, h][:, s, :],
+                    start=(s == 0),
+                    stop=(s == PASSES - 1),
+                )
+
+        def make_dx(e, h):
+            dx = dx_banks.tile([P, KT, HALF], F32, name="dx")
             for kt in range(KT):
-                dx = dx_banks.tile([P, C], F32, name="dx")
-                for h in halves:
-                    for s in range(PASSES):
-                        group = (e % 2) * PASSES + s
-                        col = (e * PASSES + s) * K + kt * P
-                        nc.tensor.matmul_mx(
-                            out=dx[:, h * HALF : (h + 1) * HALF],
-                            lhsT=w1_sb[e // 2][:, group, 2 * kt * P : 2 * (kt + 1) * P].bitcast(FP4X4),
-                            lhsT_scale=w1s_sb[:, col : col + P],
-                            rhs=da_codes[e][:, h, s, :].bitcast(FP8X4),
-                            rhs_scale=da_scales[e][:, h, s, :],
-                            start=(s == 0),
-                            stop=(s == PASSES - 1),
-                        )
-                lo, hi = halves[0] * HALF, (halves[-1] + 1) * HALF
-                nc.scalar.copy(dx_sb[kt][:, e * C + lo : e * C + hi], dx[:, lo:hi])
+                dx_passes(e, h, kt, dx[:, kt, :])
+            first = e * C + h * HALF
+            nc.scalar.copy(dx_sb[:, :, first : first + HALF], dx[:])
 
-        def expert(e):
-            for h in range(2):
-                for s in range(PASSES):
-                    make_da(e, h, s)
+        def make_dx_by_rows(e, h):
+            first = e * C + h * HALF
+            for kt in range(KT):
+                dx = dh_banks.tile([P, HALF], F32, name="dx_rows", tag="bank")
+                dx_passes(e, h, kt, dx[:])
+                nc.scalar.copy(dx_sb[:, kt, first : first + HALF], dx[:])
 
-        gather_g(0, 0)
         turn_w2_scales()
-        for t in range(1, PACK):
+        for t in range(PACK):
             gather_g(0, t)
         round_g(0)
         round_g(1)
         gather_g(1, 0)
         turn_w2(0)
-        quantize_g(0)
         gather_g(1, 1)
+        quantize_g(0)
         gather_g(1, 2)
         quantize_g(1)
         gather_g(1, 3)
-        for s in range(PASSES):
-            relu_a(0, s)
-        for s in range(PASSES):
-            relu_a(1, s)
+        relu_a(0, 0)
+        relu_a(0, 1)
+        gather_g(2, 0)
         round_g(2)
+        relu_a(1, 0)
+        gather_g(2, 1)
+        relu_a(1, 1)
         round_g(3)
-        expert(0)
-        turn_w2(1)
-        quantize_da(0, 0, 4)
-        make_dx(0, (0, 1))
-        expert(1)
-        quantize_g(2)
-        quantize_da(1, 0, 4)
-        make_dx(1, (0, 1))
-        quantize_g(3)
-        for s in range(PASSES):
-            relu_a(2, s)
-        for t in range(PACK):
-            gather_g(2, t)
-        for s in range(PASSES):
-            relu_a(3, s)
-        round_g(4)
-        round_g(5)
-        expert(2)
-        turn_w2(2)
-        quantize_da(2, 0, 4)
-        make_dx(2, (0, 1))
-        for s in range(PASSES):
-            relu_a(4, s)
-        expert(3)
-        quantize_g(4)
-        quantize_da(3, 0, 4)
-        make_dx(3, (0, 1))
-        quantize_g(5)
-        for s in range(PASSES):
-            relu_a(5, s)
-        expert(4)
         last = E - 1
-        make_da(last, 0, 0)
-        quantize_da(4, 0, 4)
-        make_dx(4, (0, 1))
-        make_da(last, 0, 1)
-        make_da(last, 1, 0)
-        quantize_da(last, 0, 2)
-        make_dx(last, (0,))
-        make_da(last, 1, 1)
-        quantize_da(last, 2, 1)
-        quantize_da(last, 3, 1)
-        make_dx(last, (1,))
+        for e in range(E):
+            make_da(e, 0, 0, nc.vector)
+            if e > 0:
+                quantize_da(e - 1, 1)
+                make_dx(e - 1, 1)
+            if e == 0:
+                gather_g(2, 2)
+            make_da(e, 0, 1, nc.vector)
+            if e + 2 < E:
+                relu_a(e + 2, 0)
+            make_da(e, 1, 0, nc.vector)
+            if e == 0:
+                gather_g(2, 3)
+                round_g(4)
+            if e == 1:
+                round_g(5)
+            quantize_da(e, 0)
+            make_dx(e, 0)
+            make_da(e, 1, 1, nc.vector)
+            if e + 2 < E:
+                relu_a(e + 2, 1)
+            if e in (0, 2):
+                turn_w2(e // 2 + 1)
+            if e + 2 < E:
+                quantize_g(e + 2)
+        quantize_da(last, 1)
+        make_dx_by_rows(last, 1)
 
-        pieces = [(0, 0, T), (1, 0, T), (2, 0, T // 2), (2, T // 2, T)]
+        pieces = [(kt, lo, lo + T // 2) for kt in range(KT - 1) for lo in (0, T // 2)]
+        pieces += [(KT - 1, 0, 2 * T // 3), (KT - 1, 2 * T // 3, T)]
         picked = {}
 
         def pick(n, r):
             kt, lo, hi = pieces[n]
-            picked[n, r] = keep.tile([P, hi - lo], F32, name=f"picked{n}_{r}")
-            nc.vector.tensor_copy(picked[n, r][:], dx_sb[kt][:].indirect(pos_sb[r][:, lo // 16 : hi // 16]))
+            if r == 0:
+                picked[n] = ring.tile([P, 2, hi - lo], F32, name="picked", tag="rows")
+            nc.vector.tensor_copy(picked[n][:, r, :], dx_sb[:, kt, :].indirect(pos_sb[r][:, lo // 16 : hi // 16]))
 
         def combine(n):
             kt, lo, hi = pieces[n]
             total = keep.tile([P, hi - lo], F32, name=f"total{n}")
-            nc.vector.tensor_tensor(total[:], picked[n, 0][:], picked[n, 1][:], ADD)
+            if kt == KT - 1:
+                nc.vector.tensor_tensor(total[:], picked[n][:, 0, :], picked[n][:, 1, :], ADD)
+            else:
+                blocks = (hi - lo) // P
+                sum_t = dh_banks.tile([P, blocks, P], F32, name="sum_t", tag="bank")
+                for b in range(blocks):
+                    for r in range(2):
+                        nc.tensor.matmul(
+                            sum_t[:, b, :],
+                            lhsT=picked[n][:, r, b * P : (b + 1) * P],
+                            rhs=ident[:],
+                            start=(r == 0),
+                            stop=(r == 1),
+                            is_transpose=True,
+                        )
+                sum_t_sb = ring.tile([P, blocks, P], F32, name="sum_t_sb")
+                nc.scalar.copy(sum_t_sb[:], sum_t[:])
+                back = dh_banks.tile([P, blocks, P], F32, name="back", tag="bank")
+                for b in range(blocks):
+                    nc.tensor.transpose(back[:, b, :], sum_t_sb[:, b, :], ident[:])
+                nc.scalar.copy(total[:], back[:].rearrange("p b n -> p (b n)"))
             nc.sync.dma_start(out[kt * P : (kt + 1) * P, lo:hi], total[:])
 
         pick(0, 0)

@@ -35,7 +35,6 @@ def tile_moe_bdx_mlp_relu2_kernel(
     with ExitStack() as ctx:
         keep = ctx.enter_context(tc.tile_pool(name="keep", bufs=1))
         ring = ctx.enter_context(tc.tile_pool(name="ring", bufs=3))
-        single = ctx.enter_context(tc.tile_pool(name="single", bufs=1))
         relu_ring = ctx.enter_context(tc.tile_pool(name="relu_ring", bufs=6))
         dh_banks = ctx.enter_context(tc.psum_pool(name="dh_banks", bufs=6))
         dx_banks = ctx.enter_context(tc.psum_pool(name="dx_banks", bufs=2))
@@ -45,8 +44,8 @@ def tile_moe_bdx_mlp_relu2_kernel(
         dy_sb = [keep.tile([P, T], F32, name=f"dy_sb{t}") for t in range(PACK)]
         gate_sb = [keep.tile([P, PAIR], F32, name=f"gate_sb{c}") for c in range(E // 2)]
         a_sb = [[keep.tile([P, PACK, PAIR], F32, name=f"a_sb{c}_{s}") for s in range(PASSES)] for c in range(E // 2)]
-        w2_raw = [keep.tile([P, 2, 2 * H], U8, name=f"w2_raw{c}") for c in range(E // 2)]
-        w2_sb = [keep.tile([P, 2, 2 * H], U8, name=f"w2_sb{c}", align_bytes=64) for c in range(E // 2)]
+        w2_raw = [keep.tile([P, 2 * H], U8, name=f"w2_raw{e}") for e in range(E)]
+        w2_sb = {}
         w1_sb = [keep.tile([P, 2 * PASSES, 2 * K], U8, name=f"w1_sb{c}", align_bytes=64) for c in range(E // 2)]
         w2s_raw = keep.tile([P, H], U8, name="w2s_raw")
         w2s_turned = keep.tile([P, H], U8, name="w2s_turned")
@@ -64,11 +63,8 @@ def tile_moe_bdx_mlp_relu2_kernel(
         def load_gate(c):
             nc.sync.dma_start(gate_sb[c][:], gate[0:P, c * PAIR : (c + 1) * PAIR])
 
-        def load_w2(c):
-            nc.sync.dma_start(
-                w2_raw[c][:].bitcast(I32),
-                w2_words[2 * c : 2 * c + 2].rearrange("e o p b -> p (e o) b").bitcast(I32),
-            )
+        def load_w2(e):
+            nc.sync.dma_start(w2_raw[e][:].bitcast(I32), w2_words[e, 0].bitcast(I32))
 
         def load_w1(c):
             nc.sync.dma_start(
@@ -88,28 +84,31 @@ def tile_moe_bdx_mlp_relu2_kernel(
         nc.vector.memset(warm[:], 0.0)
         nc.scalar.activation(warm[:, 1:2], warm[:, 0:1], RELU)
         nc.sync.dma_start(offs_sb[:], offs)
+        load_w2(0)
         nc.sync.dma_start(dy_sb[0][:], dy_rows[:, 0, :])
         load_gate(0)
         for t in range(1, PACK):
             nc.sync.dma_start(dy_sb[t][:], dy_rows[:, t, :])
         load_gate(1)
-        load_w2(0)
-        load_gate(2)
         load_a(0, 0)
+        load_w2(1)
+        load_gate(2)
         load_a(0, 1)
         for q in range(4):
             nc.sync.dma_start(
                 w1s_sb[32 * q : 32 * q + 4, :].rearrange("f (g k) -> f g k", k=K).bitcast(I32),
                 w1_scales[:, :, 4 * q : 4 * q + 4, :].rearrange("e s f k -> f (e s) k").bitcast(I32),
             )
-        load_w2(1)
+        load_w2(2)
         load_a(1, 0)
         load_a(1, 1)
         load_w1(0)
-        load_w2(2)
+        load_w2(3)
+        load_w2(4)
         for half in range(2):
             for s in range(PASSES):
                 load_a(2, s, half * C, (half + 1) * C)
+        load_w2(5)
         load_w1(1)
         load_w1(2)
         nc.sync.dma_start(pos_sb[0][:], pos1)
@@ -140,10 +139,11 @@ def tile_moe_bdx_mlp_relu2_kernel(
                 out=g_codes[e][:].bitcast(FP8X4), scales=g_scales[e][:], in_=g_bf[e][:].rearrange("p c t -> p (c t)")
             )
 
-        def turn_w2(c):
-            nc.vector.tensor_copy(
-                w2_sb[c][:].bitcast(U16).rearrange("p e (s t m) -> p (e s) t m", s=PASSES, t=PACK),
-                w2_raw[c][:].bitcast(U16).rearrange("p e (s m t) -> p (e s) t m", s=PASSES, t=PACK),
+        def turn_w2(e, engine):
+            w2_sb[e] = keep.tile([P, 2 * H], U8, name=f"w2_sb{e}", tag=f"slot{e}", align_bytes=64)
+            engine.tensor_copy(
+                w2_sb[e][:].bitcast(U16).rearrange("p (s t m) -> p s t m", s=PASSES, t=PACK),
+                w2_raw[e][:].bitcast(U16).rearrange("p (s m t) -> p s t m", s=PASSES, t=PACK),
             )
 
         def turn_w2_scales():
@@ -174,7 +174,7 @@ def tile_moe_bdx_mlp_relu2_kernel(
                 col = (s * PACK + t) * P
                 nc.tensor.matmul_mx(
                     out=dh[:, t, :],
-                    lhsT=w2_sb[e // 2][:, e % 2, 2 * col : 2 * (col + P)].bitcast(FP4X4),
+                    lhsT=w2_sb[e][:, 2 * col : 2 * (col + P)].bitcast(FP4X4),
                     lhsT_scale=w2s_sb[:, e * H + col : e * H + col + P],
                     rhs=g_codes[e][:, slots].bitcast(FP8X4),
                     rhs_scale=g_scales[e][:, slots],
@@ -183,24 +183,23 @@ def tile_moe_bdx_mlp_relu2_kernel(
                 )
             return dh[:].rearrange("p t n -> p n t")
 
-        def stage_dh(e):
-            dh_sb[e] = ring.tile([P, HALF, PACK], F32, name="dh_sb")
-            nc.scalar.copy(dh_sb[e][:], make_dh(e, 0, 0))
+        def make_da(e, h, s):
+            if s == 0:
+                tag = f"slot{e + 2}" if h == 1 else f"da_first{e % 2}"
+                da_bf[e, h] = keep.tile([P, PASSES, HALF, PACK], BF16, name=f"da_bf{e}_{h}", tag=tag, align_bytes=64)
+            nc.vector.tensor_tensor(
+                da_bf[e, h][:, s, :, :], make_dh(e, h, s), relu_sb[e, s][:, h * HALF : (h + 1) * HALF, :], MULT
+            )
 
-        def make_da(e, h, s, engine):
-            if (e, h) not in da_bf:
-                pool = ring
-                da_bf[e, h] = pool.tile([P, PASSES, HALF, PACK], BF16, name=f"da_bf{h}", align_bytes=64)
-            dh = dh_sb[e][:] if engine is nc.gpsimd else make_dh(e, h, s)
-            engine.tensor_tensor(da_bf[e, h][:, s, :, :], dh, relu_sb[e, s][:, h * HALF : (h + 1) * HALF, :], MULT)
-
-        def quantize_da(e, h):
-            da_codes[e, h] = ring.tile([P, PASSES, HALF], U32, name=f"da_codes{h}", align_bytes=64)
-            da_scales[e, h] = ring.tile([P, PASSES, HALF], U8, name=f"da_scales{h}", align_bytes=64)
+        def quantize_da(e, h, first=0, count=PASSES):
+            if first == 0:
+                da_codes[e, h] = ring.tile([P, PASSES, HALF], U32, name=f"da_codes{h}", align_bytes=64)
+                da_scales[e, h] = ring.tile([P, PASSES, HALF], U8, name=f"da_scales{h}", align_bytes=64)
+            passes = slice(first, first + count)
             nc.vector.quantize_mx(
-                out=da_codes[e, h][:].rearrange("p s n -> p (s n)").bitcast(FP8X4),
-                scales=da_scales[e, h][:].rearrange("p s n -> p (s n)"),
-                in_=da_bf[e, h][:].rearrange("p s n t -> p (s n t)"),
+                out=da_codes[e, h][:, passes, :].rearrange("p s n -> p (s n)").bitcast(FP8X4),
+                scales=da_scales[e, h][:, passes, :].rearrange("p s n -> p (s n)"),
+                in_=da_bf[e, h][:, passes, :, :].rearrange("p s n t -> p (s n t)"),
             )
 
         def dx_passes(e, h, kt, dx):
@@ -229,15 +228,18 @@ def tile_moe_bdx_mlp_relu2_kernel(
             for kt in range(KT):
                 dx = dh_banks.tile([P, HALF], F32, name="dx_rows", tag="bank")
                 dx_passes(e, h, kt, dx[:])
-                nc.scalar.copy(dx_sb[:, kt, first : first + HALF], dx[:])
+                if kt == 0:
+                    nc.vector.tensor_copy(dx_sb[:, kt, first : first + HALF], dx[:])
+                else:
+                    nc.scalar.copy(dx_sb[:, kt, first : first + HALF], dx[:])
 
         turn_w2_scales()
+        turn_w2(0, nc.vector)
         for t in range(PACK):
             gather_g(0, t)
         round_g(0)
         round_g(1)
         gather_g(1, 0)
-        turn_w2(0)
         gather_g(1, 1)
         quantize_g(0)
         gather_g(1, 2)
@@ -248,36 +250,39 @@ def tile_moe_bdx_mlp_relu2_kernel(
         gather_g(2, 0)
         round_g(2)
         relu_a(1, 0)
+        turn_w2(1, nc.vector)
         gather_g(2, 1)
         relu_a(1, 1)
         round_g(3)
         last = E - 1
-        for e in range(E):
-            make_da(e, 0, 0, nc.vector)
-            if e > 0:
-                quantize_da(e - 1, 1)
-                make_dx(e - 1, 1)
+        for e in range(last):
+            for h in range(2):
+                for s in range(PASSES):
+                    make_da(e, h, s)
             if e == 0:
                 gather_g(2, 2)
-            make_da(e, 0, 1, nc.vector)
-            if e + 2 < E:
-                relu_a(e + 2, 0)
-            make_da(e, 1, 0, nc.vector)
-            if e == 0:
                 gather_g(2, 3)
-                round_g(4)
-            if e == 1:
-                round_g(5)
-            quantize_da(e, 0)
-            make_dx(e, 0)
-            make_da(e, 1, 1, nc.vector)
-            if e + 2 < E:
-                relu_a(e + 2, 1)
-            if e in (0, 2):
-                turn_w2(e // 2 + 1)
             if e + 2 < E:
                 quantize_g(e + 2)
-        quantize_da(last, 1)
+            quantize_da(e, 0)
+            make_dx(e, 0)
+            quantize_da(e, 1)
+            make_dx(e, 1)
+            if e + 2 < E:
+                turn_w2(e + 2, nc.gpsimd)
+            if e < 2:
+                round_g(4 + e)
+            if e + 2 < E:
+                relu_a(e + 2, 0)
+                relu_a(e + 2, 1)
+        make_da(last, 0, 0)
+        make_da(last, 0, 1)
+        make_da(last, 1, 0)
+        quantize_da(last, 0)
+        make_dx(last, 0)
+        make_da(last, 1, 1)
+        quantize_da(last, 1, 0, 1)
+        quantize_da(last, 1, 1, 1)
         make_dx_by_rows(last, 1)
 
         pieces = [(kt, lo, lo + T // 2) for kt in range(KT - 1) for lo in (0, T // 2)]

@@ -35,15 +35,15 @@ def tile_moe_bdx_mlp_relu2_kernel(
     with ExitStack() as ctx:
         keep = ctx.enter_context(tc.tile_pool(name="keep", bufs=1))
         ring = ctx.enter_context(tc.tile_pool(name="ring", bufs=3))
-        relu_ring = ctx.enter_context(tc.tile_pool(name="relu_ring", bufs=6))
+        relu_ring = ctx.enter_context(tc.tile_pool(name="relu_ring", bufs=8))
         dh_banks = ctx.enter_context(tc.psum_pool(name="dh_banks", bufs=6))
         dx_banks = ctx.enter_context(tc.psum_pool(name="dx_banks", bufs=2))
 
         offs_sb = keep.tile([P, S // 16], U16, name="offs_sb")
         pos_sb = [keep.tile([P, T // 16], U16, name=f"pos_sb{r}") for r in range(2)]
-        dy_sb = [keep.tile([P, T], F32, name=f"dy_sb{t}") for t in range(PACK)]
-        gate_sb = [keep.tile([P, PAIR], F32, name=f"gate_sb{c}") for c in range(E // 2)]
-        a_sb = [[keep.tile([P, PACK, PAIR], F32, name=f"a_sb{c}_{s}") for s in range(PASSES)] for c in range(E // 2)]
+        dy_sb = [keep.tile([P, T], F32, name=f"dy_sb{t}", tag=f"dy{t}", align_bytes=64) for t in range(PACK)]
+        gate_sb = [keep.tile([P, PAIR], F32, name=f"gate_sb{c}", tag=f"gate{c}", align_bytes=64) for c in range(E // 2)]
+        a_sb = [[keep.tile([P, PACK, PAIR], F32, name=f"a_sb{c}_{s}", tag=f"a{PASSES * c + s}") for s in range(PASSES)] for c in range(E // 2)]
         w2_raw = [keep.tile([P, 2 * H], U8, name=f"w2_raw{e}") for e in range(E)]
         w2_sb = {}
         w1_sb = [keep.tile([P, 2 * PASSES, 2 * K], U8, name=f"w1_sb{c}", align_bytes=64) for c in range(E // 2)]
@@ -91,56 +91,58 @@ def tile_moe_bdx_mlp_relu2_kernel(
             nc.sync.dma_start(dy_sb[t][:], dy_rows[:, t, :])
         load_gate(1)
         load_a(0, 0)
-        load_w2(1)
-        load_gate(2)
         load_a(0, 1)
+        load_gate(2)
+        load_a(1, 0)
+        load_w2(1)
+        load_w2(2)
+        load_a(1, 1)
         for q in range(4):
             nc.sync.dma_start(
                 w1s_sb[32 * q : 32 * q + 4, :].rearrange("f (g k) -> f g k", k=K).bitcast(I32),
                 w1_scales[:, :, 4 * q : 4 * q + 4, :].rearrange("e s f k -> f (e s) k").bitcast(I32),
             )
-        load_w2(2)
-        load_a(1, 0)
-        load_a(1, 1)
         load_w1(0)
         load_w2(3)
-        load_w2(4)
+        load_w1(1)
         for half in range(2):
             for s in range(PASSES):
                 load_a(2, s, half * C, (half + 1) * C)
-        load_w2(5)
-        load_w1(1)
+            load_w2(4 + half)
         load_w1(2)
         nc.sync.dma_start(pos_sb[0][:], pos1)
         nc.sync.dma_start(pos_sb[1][:], pos2)
 
         g_rows, g_bf, g_codes, g_scales = {}, {}, {}, {}
-        relu_sb, dh_sb, da_bf, da_codes, da_scales = {}, {}, {}, {}, {}
+        relu_sb, dh_first, dh_sb, da_bf, da_codes, da_scales = {}, {}, {}, {}, {}, {}
 
         def gather_g(c, t):
             if t == 0:
-                g_rows[c] = ring.tile([P, PACK, PAIR], F32, name="g_rows", tag="rows")
+                g_rows[c] = ring.tile([P, PACK, PAIR], F32, name="g_rows")
             cols = PAIR // 16
             nc.vector.tensor_tensor(
                 g_rows[c][:, t, :], dy_sb[t][:].indirect(offs_sb[:, c * cols : (c + 1) * cols]), gate_sb[c][:], MULT
             )
 
         def round_g(e):
-            g_bf[e] = keep.tile([P, C, PACK], BF16, name=f"g_bf{e}", align_bytes=64)
-            src = g_rows[e // 2][:, :, (e % 2) * C : (e % 2 + 1) * C]
+            if e % 2 == 0:
+                g_bf[e // 2] = keep.tile([P, PAIR, PACK], BF16, name=f"g_bf{e // 2}", align_bytes=64)
+            slots = slice((e % 2) * C, (e % 2 + 1) * C)
             nc.scalar.copy(
-                g_bf[e][:].rearrange("p (c i) t -> p c t i", i=2), src.rearrange("p t (c i) -> p c t i", i=2)
+                g_bf[e // 2][:, slots, :].rearrange("p (c i) t -> p c t i", i=2),
+                g_rows[e // 2][:, :, slots].rearrange("p t (c i) -> p c t i", i=2),
             )
 
-        def quantize_g(e):
-            g_codes[e] = keep.tile([P, C], U32, name=f"g_codes{e}", align_bytes=64)
-            g_scales[e] = keep.tile([P, C], U8, name=f"g_scales{e}", align_bytes=64)
+        def quantize_g(c):
+            g_codes[c] = keep.tile([P, PAIR], U32, name=f"g_codes{c}", align_bytes=64)
+            g_scales[c] = keep.tile([P, PAIR], U8, name=f"g_scales{c}", align_bytes=64)
             nc.vector.quantize_mx(
-                out=g_codes[e][:].bitcast(FP8X4), scales=g_scales[e][:], in_=g_bf[e][:].rearrange("p c t -> p (c t)")
+                out=g_codes[c][:].bitcast(FP8X4), scales=g_scales[c][:], in_=g_bf[c][:].rearrange("p c t -> p (c t)")
             )
 
         def turn_w2(e, engine):
-            w2_sb[e] = keep.tile([P, 2 * H], U8, name=f"w2_sb{e}", tag=f"slot{e}", align_bytes=64)
+            tag = {1: f"dy{PACK - 1}", 2: f"gate{E // 2 - 1}"}.get(e, f"slot{e}")
+            w2_sb[e] = keep.tile([P, 2 * H], U8, name=f"w2_sb{e}", tag=tag, align_bytes=64)
             engine.tensor_copy(
                 w2_sb[e][:].bitcast(U16).rearrange("p (s t m) -> p s t m", s=PASSES, t=PACK),
                 w2_raw[e][:].bitcast(U16).rearrange("p (s m t) -> p s t m", s=PASSES, t=PACK),
@@ -169,26 +171,49 @@ def tile_moe_bdx_mlp_relu2_kernel(
 
         def make_dh(e, h, s):
             dh = dh_banks.tile([P, PACK, HALF], F32, name="dh", tag="bank")
-            slots = slice(h * HALF, (h + 1) * HALF)
+            first = (e % 2) * C + h * HALF
+            slots = slice(first, first + HALF)
             for t in range(PACK):
                 col = (s * PACK + t) * P
                 nc.tensor.matmul_mx(
                     out=dh[:, t, :],
                     lhsT=w2_sb[e][:, 2 * col : 2 * (col + P)].bitcast(FP4X4),
                     lhsT_scale=w2s_sb[:, e * H + col : e * H + col + P],
-                    rhs=g_codes[e][:, slots].bitcast(FP8X4),
-                    rhs_scale=g_scales[e][:, slots],
+                    rhs=g_codes[e // 2][:, slots].bitcast(FP8X4),
+                    rhs_scale=g_scales[e // 2][:, slots],
                     start=True,
                     stop=True,
                 )
             return dh[:].rearrange("p t n -> p n t")
 
-        def make_da(e, h, s):
-            if s == 0:
-                tag = f"slot{e + 2}" if h == 1 else f"da_first{e % 2}"
+        def da_tile(e, h):
+            if (e, h) not in da_bf:
+                tag = f"slot{e + 3}" if h == 1 else "da_first"
                 da_bf[e, h] = keep.tile([P, PASSES, HALF, PACK], BF16, name=f"da_bf{e}_{h}", tag=tag, align_bytes=64)
+            return da_bf[e, h]
+
+        def make_da(e, h, s):
             nc.vector.tensor_tensor(
-                da_bf[e, h][:, s, :, :], make_dh(e, h, s), relu_sb[e, s][:, h * HALF : (h + 1) * HALF, :], MULT
+                da_tile(e, h)[:, s, :, :], make_dh(e, h, s), relu_sb[e, s][:, h * HALF : (h + 1) * HALF, :], MULT
+            )
+
+        def shared_slots(e):
+            return HALF // 2 if e == E - 1 else HALF
+
+        def stage_dh(e):
+            n = shared_slots(e)
+            dh_first[e] = make_dh(e, 0, 0)
+            dh_sb[e] = ring.tile([P, n, PACK], F32, name="dh_sb")
+            nc.scalar.copy(dh_sb[e][:], dh_first[e][:, 0:n, :])
+
+        def make_da_gpsimd(e):
+            n = shared_slots(e)
+            nc.gpsimd.tensor_tensor(da_tile(e, 0)[:, 0, 0:n, :], dh_sb[e][:], relu_sb[e, 0][:, 0:n, :], MULT)
+
+        def make_da_rest(e):
+            n = shared_slots(e)
+            nc.vector.tensor_tensor(
+                da_tile(e, 0)[:, 0, n:HALF, :], dh_first[e][:, n:HALF, :], relu_sb[e, 0][:, n:HALF, :], MULT
             )
 
         def quantize_da(e, h, first=0, count=PASSES):
@@ -239,66 +264,74 @@ def tile_moe_bdx_mlp_relu2_kernel(
             gather_g(0, t)
         round_g(0)
         round_g(1)
-        gather_g(1, 0)
-        gather_g(1, 1)
+        for t in range(PACK):
+            gather_g(1, t)
         quantize_g(0)
-        gather_g(1, 2)
-        quantize_g(1)
-        gather_g(1, 3)
         relu_a(0, 0)
         relu_a(0, 1)
-        gather_g(2, 0)
         round_g(2)
-        relu_a(1, 0)
-        turn_w2(1, nc.vector)
-        gather_g(2, 1)
-        relu_a(1, 1)
         round_g(3)
+        for t in range(PACK - 1):
+            gather_g(2, t)
+        quantize_g(1)
+        gather_g(2, PACK - 1)
+        for e in (1, 2):
+            relu_a(e, 0)
+            relu_a(e, 1)
         last = E - 1
+        turn_w2(1, nc.gpsimd)
+        turn_w2(2, nc.gpsimd)
+        make_da(0, 1, 0)
         for e in range(last):
-            for h in range(2):
-                for s in range(PASSES):
-                    make_da(e, h, s)
-            if e == 0:
-                gather_g(2, 2)
-                gather_g(2, 3)
-            if e + 2 < E:
-                quantize_g(e + 2)
-            quantize_da(e, 0)
-            make_dx(e, 0)
+            make_da(e, 1, 1)
+            if e == last - 1:
+                make_da_gpsimd(e)
+            else:
+                make_da(e, 0, 0)
+            make_da(e, 0, 1)
+            make_da(e + 1, 1, 0)
+            if e + 1 >= last - 1:
+                stage_dh(e + 1)
+            if e == 1:
+                quantize_g(2)
             quantize_da(e, 1)
+            quantize_da(e, 0)
+            if e + 3 < E:
+                turn_w2(e + 3, nc.gpsimd)
             make_dx(e, 1)
-            if e + 2 < E:
-                turn_w2(e + 2, nc.gpsimd)
-            if e < 2:
-                round_g(4 + e)
-            if e + 2 < E:
-                relu_a(e + 2, 0)
-                relu_a(e + 2, 1)
-        make_da(last, 0, 0)
+            make_dx(e, 0)
+            if e == 0:
+                round_g(4)
+                round_g(5)
+            if e + 3 < E:
+                relu_a(e + 3, 0)
+                relu_a(e + 3, 1)
+        make_da_gpsimd(last)
+        make_da_rest(last)
         make_da(last, 0, 1)
-        make_da(last, 1, 0)
+        quantize_da(last, 1, 0, 1)
         quantize_da(last, 0)
         make_dx(last, 0)
         make_da(last, 1, 1)
-        quantize_da(last, 1, 0, 1)
         quantize_da(last, 1, 1, 1)
         make_dx_by_rows(last, 1)
 
-        pieces = [(kt, lo, lo + T // 2) for kt in range(KT - 1) for lo in (0, T // 2)]
-        pieces += [(KT - 1, 0, 2 * T // 3), (KT - 1, 2 * T // 3, T)]
+        pieces = [(0, 0, T // 2), (0, T // 2, T)]
+        pieces += [(kt, lo, hi) for kt in (1, 2) for lo, hi in ((0, 2 * T // 3), (2 * T // 3, T))]
+        on_tensor = 3
         picked = {}
 
         def pick(n, r):
             kt, lo, hi = pieces[n]
             if r == 0:
-                picked[n] = ring.tile([P, 2, hi - lo], F32, name="picked", tag="rows")
+                picked[n] = keep.tile([P, 2, hi - lo], F32, name=f"picked{n}", tag=f"a{n}")
             nc.vector.tensor_copy(picked[n][:, r, :], dx_sb[:, kt, :].indirect(pos_sb[r][:, lo // 16 : hi // 16]))
 
         def combine(n):
             kt, lo, hi = pieces[n]
-            total = keep.tile([P, hi - lo], F32, name=f"total{n}")
-            if kt == KT - 1:
+            tag = f"dy{n}" if n < 3 else f"gate{n - 3}"
+            total = keep.tile([P, hi - lo], F32, name=f"total{n}", tag=tag, align_bytes=64)
+            if n >= on_tensor:
                 nc.vector.tensor_tensor(total[:], picked[n][:, 0, :], picked[n][:, 1, :], ADD)
             else:
                 blocks = (hi - lo) // P
@@ -319,7 +352,8 @@ def tile_moe_bdx_mlp_relu2_kernel(
                 for b in range(blocks):
                     nc.tensor.transpose(back[:, b, :], sum_t_sb[:, b, :], ident[:])
                 nc.scalar.copy(total[:], back[:].rearrange("p b n -> p (b n)"))
-            nc.sync.dma_start(out[kt * P : (kt + 1) * P, lo:hi], total[:])
+            queue = nc.sync if n >= on_tensor else nc.scalar
+            queue.dma_start(out[kt * P : (kt + 1) * P, lo:hi], total[:])
 
         pick(0, 0)
         pick(0, 1)

@@ -54,14 +54,18 @@ def tile_moe_bdx_mlp_relu2_kernel(
         dx_sb = keep.tile([P, KT, S], F32, name="dx_sb")
         warm = keep.tile([P, 2], F32, name="warm")
 
+        gate_cols = keep.tile([P, E // 2, PACK], F32, name="gate_cols")
         ident = keep.tile([P, P], F32, name="ident")
         make_identity(nc, ident[:])
 
         dy_rows = dyT.rearrange("(p t) j -> p t j", t=PACK)
         a_rows = a.rearrange("(s p t) j -> s p t j", s=PASSES, t=PACK)
 
-        def load_gate(c):
-            nc.sync.dma_start(gate_sb[c][:], gate[0:P, c * PAIR : (c + 1) * PAIR])
+        def spread_gate(c):
+            bank = dh_banks.tile([P, PACK, P], F32, name="gate_bank", tag="bank")
+            for m in range(PACK):
+                nc.tensor.transpose(bank[:, m, :], gate_cols[:, c, m : m + 1].to_broadcast([P, P]), ident[:])
+            nc.scalar.copy(gate_sb[c][:].rearrange("p (n m) -> p n m", m=PACK), bank[:].rearrange("p m n -> p n m"))
 
         def load_w2(e):
             nc.sync.dma_start(w2_raw[e][:].bitcast(I32), w2_words[e, 0].bitcast(I32))
@@ -83,19 +87,16 @@ def tile_moe_bdx_mlp_relu2_kernel(
         )
         nc.vector.memset(warm[:], 0.0)
         nc.scalar.activation(warm[:, 1:2], warm[:, 0:1], RELU)
+        nc.sync.dma_start(gate_cols[:], gate[0].rearrange("(c n m) -> n c m", c=E // 2, m=PACK))
         nc.sync.dma_start(offs_sb[:], offs)
         load_w2(0)
-        nc.sync.dma_start(dy_sb[0][:], dy_rows[:, 0, :])
-        load_gate(0)
-        for t in range(1, PACK):
+        load_w2(1)
+        for t in range(PACK):
             nc.sync.dma_start(dy_sb[t][:], dy_rows[:, t, :])
-        load_gate(1)
         load_a(0, 0)
         load_a(0, 1)
-        load_gate(2)
-        load_a(1, 0)
-        load_w2(1)
         load_w2(2)
+        load_a(1, 0)
         load_a(1, 1)
         for q in range(4):
             nc.sync.dma_start(
@@ -141,7 +142,7 @@ def tile_moe_bdx_mlp_relu2_kernel(
             )
 
         def turn_w2(e, engine):
-            tag = {1: f"dy{PACK - 1}", 2: f"gate{E // 2 - 1}"}.get(e, f"slot{e}")
+            tag = f"gate{E // 2 - 1}" if e == 2 else f"slot{e}"
             w2_sb[e] = keep.tile([P, 2 * H], U8, name=f"w2_sb{e}", tag=tag, align_bytes=64)
             engine.tensor_copy(
                 w2_sb[e][:].bitcast(U16).rearrange("p (s t m) -> p s t m", s=PASSES, t=PACK),
@@ -259,7 +260,10 @@ def tile_moe_bdx_mlp_relu2_kernel(
                     nc.scalar.copy(dx_sb[:, kt, first : first + HALF], dx[:])
 
         turn_w2_scales()
+        for c in range(E // 2):
+            spread_gate(c)
         turn_w2(0, nc.vector)
+        turn_w2(1, nc.vector)
         for t in range(PACK):
             gather_g(0, t)
         round_g(0)
@@ -279,7 +283,6 @@ def tile_moe_bdx_mlp_relu2_kernel(
             relu_a(e, 0)
             relu_a(e, 1)
         last = E - 1
-        turn_w2(1, nc.gpsimd)
         turn_w2(2, nc.gpsimd)
         make_da(0, 1, 0)
         for e in range(last):

from contextlib import ExitStack

import concourse.mybir as mybir
from concourse.masks import make_identity

K, T, E, C, H, N = 384, 768, 6, 256, 1024, 512
S = E * C
P = 128
PACK = 4
PASSES = H // (P * PACK)
KT = K // P
PAIR = 2 * C
HALF = 128

F32 = mybir.dt.float32
BF16 = mybir.dt.bfloat16
I32 = mybir.dt.int32
U32 = mybir.dt.uint32
U16 = mybir.dt.uint16
U8 = mybir.dt.uint8
FP8X4 = mybir.dt.float8_e4m3fn_x4
FP4X4 = mybir.dt.float4_e2m1fn_x4
MULT = mybir.AluOpType.mult
ADD = mybir.AluOpType.add
RELU = mybir.ActivationFunctionType.Relu

FLOPS = 2 * S * (N * H + H * K)
BYTES = 4 * (N * T + H * S + S + K * T) + E * (N * H + H * K) // 2 + E * (N * H + H * K) // 32 + 2 * P * (S + 2 * T) // 16


def tile_moe_bdx_mlp_relu2_kernel(
    tc, dyT, a, w2_words, w2_scales, w1_words, w1_scales, gate, offs, pos1, pos2, out
):
    nc = tc.nc
    with ExitStack() as ctx:
        keep = ctx.enter_context(tc.tile_pool(name="keep", bufs=1))
        ring = ctx.enter_context(tc.tile_pool(name="ring", bufs=3))
        relu_ring = ctx.enter_context(tc.tile_pool(name="relu_ring", bufs=8))
        dh_banks = ctx.enter_context(tc.psum_pool(name="dh_banks", bufs=6))
        dx_banks = ctx.enter_context(tc.psum_pool(name="dx_banks", bufs=2))

        offs_sb = keep.tile([P, S // 16], U16, name="offs_sb")
        pos_sb = [keep.tile([P, T // 16], U16, name=f"pos_sb{r}") for r in range(2)]
        dy_sb = [keep.tile([P, T], F32, name=f"dy_sb{t}", tag=f"dy{t}", align_bytes=64) for t in range(PACK)]
        gate_sb = [keep.tile([P, PAIR], F32, name=f"gate_sb{c}", tag=f"gate{c}", align_bytes=64) for c in range(E // 2)]
        a_sb = [[keep.tile([P, PACK, PAIR], F32, name=f"a_sb{c}_{s}", tag=f"a{PASSES * c + s}") for s in range(PASSES)] for c in range(E // 2)]
        w2_raw = [keep.tile([P, 2 * H], U8, name=f"w2_raw{e}") for e in range(E)]
        w2_sb = {}
        w1_sb = [keep.tile([P, 2 * PASSES, 2 * K], U8, name=f"w1_sb{c}", align_bytes=64) for c in range(E // 2)]
        w2s_raw = keep.tile([P, H], U8, name="w2s_raw")
        w2s_turned = keep.tile([P, H], U8, name="w2s_turned")
        w2s_sb = keep.tile([P, E * H], U8, name="w2s_sb", align_bytes=64)
        w1s_sb = keep.tile([P, E * PASSES * K], U8, name="w1s_sb", align_bytes=64)
        dx_sb = keep.tile([P, KT, S], F32, name="dx_sb")
        warm = keep.tile([P, 2], F32, name="warm")

        gate_cols = keep.tile([P, E // 2, PACK], F32, name="gate_cols")
        ident = keep.tile([P, P], F32, name="ident")
        make_identity(nc, ident[:])

        dy_rows = dyT.rearrange("(p t) j -> p t j", t=PACK)
        a_rows = a.rearrange("(s p t) j -> s p t j", s=PASSES, t=PACK)

        def spread_gate(c):
            bank = dh_banks.tile([P, PACK, P], F32, name="gate_bank", tag="bank")
            for m in range(PACK):
                nc.tensor.transpose(bank[:, m, :], gate_cols[:, c, m : m + 1].to_broadcast([P, P]), ident[:])
            nc.scalar.copy(gate_sb[c][:].rearrange("p (n m) -> p n m", m=PACK), bank[:].rearrange("p m n -> p n m"))

        def load_w2(e):
            nc.sync.dma_start(w2_raw[e][:].bitcast(I32), w2_words[e, 0].bitcast(I32))

        def load_w1(c):
            nc.sync.dma_start(
                w1_sb[c][:].bitcast(I32),
                w1_words[2 * c : 2 * c + 2].rearrange("e s p b -> p (e s) b").bitcast(I32),
            )

        def load_a(c, s, lo=0, hi=PAIR):
            nc.sync.dma_start(a_sb[c][s][:, :, lo:hi], a_rows[s][:, :, c * PAIR + lo : c * PAIR + hi])

        nc.vector.memset(w2s_raw[96:P, :].bitcast(I32), 0)
        nc.vector.memset(w2s_sb[:].bitcast(I32), 0)
        nc.vector.memset(w1s_sb[:].bitcast(I32), 0)
        nc.scalar.dma_start(
            w2s_raw[0 : 16 * E, :].bitcast(I32), w2_scales.rearrange("e o f i -> f (e o) i").bitcast(I32)
        )
        nc.vector.memset(warm[:], 0.0)
        nc.scalar.activation(warm[:, 1:2], warm[:, 0:1], RELU)
        nc.sync.dma_start(gate_cols[:], gate[0].rearrange("(c n m) -> n c m", c=E // 2, m=PACK))
        nc.sync.dma_start(offs_sb[:], offs)
        load_w2(0)
        load_w2(1)
        for t in range(PACK):
            nc.sync.dma_start(dy_sb[t][:], dy_rows[:, t, :])
        load_a(0, 0)
        load_a(0, 1)
        load_w2(2)
        load_a(1, 0)
        load_a(1, 1)
        for q in range(4):
            nc.sync.dma_start(
                w1s_sb[32 * q : 32 * q + 4, :].rearrange("f (g k) -> f g k", k=K).bitcast(I32),
                w1_scales[:, :, 4 * q : 4 * q + 4, :].rearrange("e s f k -> f (e s) k").bitcast(I32),
            )
        load_w1(0)
        load_w2(3)
        load_w1(1)
        for half in range(2):
            for s in range(PASSES):
                load_a(2, s, half * C, (half + 1) * C)
            load_w2(4 + half)
        load_w1(2)
        nc.sync.dma_start(pos_sb[0][:], pos1)
        nc.sync.dma_start(pos_sb[1][:], pos2)

        g_rows, g_bf, g_codes, g_scales = {}, {}, {}, {}
        relu_sb, dh_first, dh_sb, da_bf, da_codes, da_scales = {}, {}, {}, {}, {}, {}

        def gather_g(c, t):
            if t == 0:
                g_rows[c] = ring.tile([P, PACK, PAIR], F32, name="g_rows")
            cols = PAIR // 16
            nc.vector.tensor_tensor(
                g_rows[c][:, t, :], dy_sb[t][:].indirect(offs_sb[:, c * cols : (c + 1) * cols]), gate_sb[c][:], MULT
            )

        def round_g(e):
            if e % 2 == 0:
                g_bf[e // 2] = keep.tile([P, PAIR, PACK], BF16, name=f"g_bf{e // 2}", align_bytes=64)
            slots = slice((e % 2) * C, (e % 2 + 1) * C)
            nc.scalar.copy(
                g_bf[e // 2][:, slots, :].rearrange("p (c i) t -> p c t i", i=2),
                g_rows[e // 2][:, :, slots].rearrange("p t (c i) -> p c t i", i=2),
            )

        def quantize_g(c):
            g_codes[c] = keep.tile([P, PAIR], U32, name=f"g_codes{c}", align_bytes=64)
            g_scales[c] = keep.tile([P, PAIR], U8, name=f"g_scales{c}", align_bytes=64)
            nc.vector.quantize_mx(
                out=g_codes[c][:].bitcast(FP8X4), scales=g_scales[c][:], in_=g_bf[c][:].rearrange("p c t -> p (c t)")
            )

        def turn_w2(e, engine):
            tag = f"gate{E // 2 - 1}" if e == 2 else f"slot{e}"
            w2_sb[e] = keep.tile([P, 2 * H], U8, name=f"w2_sb{e}", tag=tag, align_bytes=64)
            engine.tensor_copy(
                w2_sb[e][:].bitcast(U16).rearrange("p (s t m) -> p s t m", s=PASSES, t=PACK),
                w2_raw[e][:].bitcast(U16).rearrange("p (s m t) -> p s t m", s=PASSES, t=PACK),
            )

        def turn_w2_scales():
            nc.vector.tensor_copy(
                w2s_turned[:].rearrange("p (s t m) -> p s t m", s=PASSES, t=PACK),
                w2s_raw[:].rearrange("p (s m t) -> p s t m", s=PASSES, t=PACK),
            )
            for q in range(4):
                nc.gpsimd.dma_start(
                    w2s_sb[32 * q : 32 * q + 4, :].bitcast(I32),
                    w2s_turned[4 * E * q : 4 * E * (q + 1), :].bitcast(I32),
                )

        def relu_a(e, s):
            relu_sb[e, s] = relu_ring.tile([P, C, PACK], F32, name="relu_sb")
            src = a_sb[e // 2][s][:, :, (e % 2) * C : (e % 2 + 1) * C]
            nc.scalar.activation(
                relu_sb[e, s][:].rearrange("p (c i) t -> p c t i", i=2),
                src.rearrange("p t (c i) -> p c t i", i=2),
                RELU,
                scale=2.0,
            )

        def make_dh(e, h, s):
            dh = dh_banks.tile([P, PACK, HALF], F32, name="dh", tag="bank")
            first = (e % 2) * C + h * HALF
            slots = slice(first, first + HALF)
            for t in range(PACK):
                col = (s * PACK + t) * P
                nc.tensor.matmul_mx(
                    out=dh[:, t, :],
                    lhsT=w2_sb[e][:, 2 * col : 2 * (col + P)].bitcast(FP4X4),
                    lhsT_scale=w2s_sb[:, e * H + col : e * H + col + P],
                    rhs=g_codes[e // 2][:, slots].bitcast(FP8X4),
                    rhs_scale=g_scales[e // 2][:, slots],
                    start=True,
                    stop=True,
                )
            return dh[:].rearrange("p t n -> p n t")

        def da_tile(e, h):
            if (e, h) not in da_bf:
                tag = f"slot{e + 3}" if h == 1 else "da_first"
                da_bf[e, h] = keep.tile([P, PASSES, HALF, PACK], BF16, name=f"da_bf{e}_{h}", tag=tag, align_bytes=64)
            return da_bf[e, h]

        def make_da(e, h, s):
            nc.vector.tensor_tensor(
                da_tile(e, h)[:, s, :, :], make_dh(e, h, s), relu_sb[e, s][:, h * HALF : (h + 1) * HALF, :], MULT
            )

        def shared_slots(e):
            return HALF // 2 if e == E - 1 else HALF

        def stage_dh(e):
            n = shared_slots(e)
            dh_first[e] = make_dh(e, 0, 0)
            dh_sb[e] = ring.tile([P, n, PACK], F32, name="dh_sb")
            nc.scalar.copy(dh_sb[e][:], dh_first[e][:, 0:n, :])

        def make_da_gpsimd(e):
            n = shared_slots(e)
            nc.gpsimd.tensor_tensor(da_tile(e, 0)[:, 0, 0:n, :], dh_sb[e][:], relu_sb[e, 0][:, 0:n, :], MULT)

        def make_da_rest(e):
            n = shared_slots(e)
            nc.vector.tensor_tensor(
                da_tile(e, 0)[:, 0, n:HALF, :], dh_first[e][:, n:HALF, :], relu_sb[e, 0][:, n:HALF, :], MULT
            )

        def quantize_da(e, h, first=0, count=PASSES):
            if first == 0:
                da_codes[e, h] = ring.tile([P, PASSES, HALF], U32, name=f"da_codes{h}", align_bytes=64)
                da_scales[e, h] = ring.tile([P, PASSES, HALF], U8, name=f"da_scales{h}", align_bytes=64)
            passes = slice(first, first + count)
            nc.vector.quantize_mx(
                out=da_codes[e, h][:, passes, :].rearrange("p s n -> p (s n)").bitcast(FP8X4),
                scales=da_scales[e, h][:, passes, :].rearrange("p s n -> p (s n)"),
                in_=da_bf[e, h][:, passes, :, :].rearrange("p s n t -> p (s n t)"),
            )

        def dx_passes(e, h, kt, dx):
            for s in range(PASSES):
                group = (e % 2) * PASSES + s
                col = (e * PASSES + s) * K + kt * P
                nc.tensor.matmul_mx(
                    out=dx,
                    lhsT=w1_sb[e // 2][:, group, 2 * kt * P : 2 * (kt + 1) * P].bitcast(FP4X4),
                    lhsT_scale=w1s_sb[:, col : col + P],
                    rhs=da_codes[e, h][:, s, :].bitcast(FP8X4),
                    rhs_scale=da_scales[e, h][:, s, :],
                    start=(s == 0),
                    stop=(s == PASSES - 1),
                )

        def make_dx(e, h):
            dx = dx_banks.tile([P, KT, HALF], F32, name="dx")
            for kt in range(KT):
                dx_passes(e, h, kt, dx[:, kt, :])
            first = e * C + h * HALF
            nc.scalar.copy(dx_sb[:, :, first : first + HALF], dx[:])

        def make_dx_by_rows(e, h):
            first = e * C + h * HALF
            for kt in range(KT):
                dx = dh_banks.tile([P, HALF], F32, name="dx_rows", tag="bank")
                dx_passes(e, h, kt, dx[:])
                if kt == 0:
                    nc.vector.tensor_copy(dx_sb[:, kt, first : first + HALF], dx[:])
                else:
                    nc.scalar.copy(dx_sb[:, kt, first : first + HALF], dx[:])

        turn_w2_scales()
        for c in range(E // 2):
            spread_gate(c)
        turn_w2(0, nc.vector)
        turn_w2(1, nc.vector)
        for t in range(PACK):
            gather_g(0, t)
        round_g(0)
        round_g(1)
        for t in range(PACK):
            gather_g(1, t)
        quantize_g(0)
        relu_a(0, 0)
        relu_a(0, 1)
        round_g(2)
        round_g(3)
        for t in range(PACK - 1):
            gather_g(2, t)
        quantize_g(1)
        gather_g(2, PACK - 1)
        for e in (1, 2):
            relu_a(e, 0)
            relu_a(e, 1)
        last = E - 1
        turn_w2(2, nc.gpsimd)
        make_da(0, 1, 0)
        for e in range(last):
            make_da(e, 1, 1)
            if e == last - 1:
                make_da_gpsimd(e)
            else:
                make_da(e, 0, 0)
            make_da(e, 0, 1)
            make_da(e + 1, 1, 0)
            if e + 1 >= last - 1:
                stage_dh(e + 1)
            if e == 1:
                quantize_g(2)
            quantize_da(e, 1)
            quantize_da(e, 0)
            if e + 3 < E:
                turn_w2(e + 3, nc.gpsimd)
            make_dx(e, 1)
            make_dx(e, 0)
            if e == 0:
                round_g(4)
                round_g(5)
            if e + 3 < E:
                relu_a(e + 3, 0)
                relu_a(e + 3, 1)
        make_da_gpsimd(last)
        make_da_rest(last)
        make_da(last, 0, 1)
        quantize_da(last, 1, 0, 1)
        quantize_da(last, 0)
        make_dx(last, 0)
        make_da(last, 1, 1)
        quantize_da(last, 1, 1, 1)
        make_dx_by_rows(last, 1)

        pieces = [(0, 0, T // 2), (0, T // 2, T)]
        pieces += [(kt, lo, hi) for kt in (1, 2) for lo, hi in ((0, 2 * T // 3), (2 * T // 3, T))]
        on_tensor = 3
        picked = {}

        def pick(n, r):
            kt, lo, hi = pieces[n]
            if r == 0:
                picked[n] = keep.tile([P, 2, hi - lo], F32, name=f"picked{n}", tag=f"a{n}")
            nc.vector.tensor_copy(picked[n][:, r, :], dx_sb[:, kt, :].indirect(pos_sb[r][:, lo // 16 : hi // 16]))

        def combine(n):
            kt, lo, hi = pieces[n]
            tag = f"dy{n}" if n < 3 else f"gate{n - 3}"
            total = keep.tile([P, hi - lo], F32, name=f"total{n}", tag=tag, align_bytes=64)
            if n >= on_tensor:
                nc.vector.tensor_tensor(total[:], picked[n][:, 0, :], picked[n][:, 1, :], ADD)
            else:
                blocks = (hi - lo) // P
                sum_t = dh_banks.tile([P, blocks, P], F32, name="sum_t", tag="bank")
                for b in range(blocks):
                    for r in range(2):
                        nc.tensor.matmul(
                            sum_t[:, b, :],
                            lhsT=picked[n][:, r, b * P : (b + 1) * P],
                            rhs=ident[:],
                            start=(r == 0),
                            stop=(r == 1),
                            is_transpose=True,
                        )
                sum_t_sb = ring.tile([P, blocks, P], F32, name="sum_t_sb")
                nc.scalar.copy(sum_t_sb[:], sum_t[:])
                back = dh_banks.tile([P, blocks, P], F32, name="back", tag="bank")
                for b in range(blocks):
                    nc.tensor.transpose(back[:, b, :], sum_t_sb[:, b, :], ident[:])
                nc.scalar.copy(total[:], back[:].rearrange("p b n -> p (b n)"))
            queue = nc.sync if n >= on_tensor else nc.scalar
            queue.dma_start(out[kt * P : (kt + 1) * P, lo:hi], total[:])

        pick(0, 0)
        pick(0, 1)
        for n in range(1, len(pieces)):
            pick(n, 0)
            combine(n - 1)
            pick(n, 1)
        combine(len(pieces) - 1)
